import numpy as np
import ml_dtypes


def mxq(x, axis, fmt="e4m3"):
    dtype, down = {"e4m3": (ml_dtypes.float8_e4m3fn, 7), "e5m2": (ml_dtypes.float8_e5m2, 14)}[fmt]
    v = np.moveaxis(np.asarray(x, np.float32).astype(ml_dtypes.bfloat16).astype(np.float64), axis, -1)
    blocks = v.reshape(v.shape[:-1] + (-1, 32))
    amax = np.abs(blocks).max(-1, keepdims=True)
    byte = np.maximum(np.where(amax > 0, np.frexp(amax)[1] - 1 + 127, 0) - down, 1)
    scale = np.exp2(byte - 127.0)
    codes = (blocks / scale).astype(np.float32).astype(dtype).astype(np.float64)
    return np.moveaxis((codes * scale).reshape(v.shape), -1, axis)


WIDE = False


def mx_kscale(k):
    if not WIDE:
        return np.ones(k)
    levels = np.array([10, -10, 5, -5, 0])
    if k % 512:
        return np.exp2(np.random.permutation(np.resize(levels, k // 32))).repeat(32)
    a = np.empty((k // 512, 16))
    for p in range(k // 512):
        a[p, :8] = np.random.permutation(np.resize(levels, 8))
        for g in range(8):
            far = levels[np.abs(levels - a[p, g]) >= 10]
            a[p, g + 8] = far[np.random.randint(len(far))]
    return np.exp2(a.ravel()).repeat(32)


def f64(x):
    return np.asarray(x).astype(np.float64)


def striped(idx):
    return np.tile(np.asarray(idx).reshape(-1, 16).T, (8, 1)).astype(np.uint16)


def unstriped(offs):
    return offs[:16].T.reshape(-1).astype(np.int64)


def striped8(idx):
    return np.asarray(idx).reshape(8, -1, 16).transpose(0, 2, 1).reshape(128, -1).astype(np.uint16)


def unstriped8(offs):
    return offs.reshape(8, 16, -1).transpose(0, 2, 1).reshape(8, -1).astype(np.int64)


def pick8(x, idx, run):
    r = np.arange(len(x))
    return x[r[:, None], idx[r % (8 * run) // run]]


E2M1 = np.array([0.0, 0.5, 1.0, 1.5, 2.0, 3.0, 4.0, 6.0, -0.0, -0.5, -1.0, -1.5, -2.0, -3.0, -4.0, -6.0])


def pack_weight(w, fmt):
    k, n = w.shape
    w = f64(np.asarray(w, np.float32).astype(ml_dtypes.bfloat16)).reshape(k // 32, 32, n)
    amax = np.abs(w).max(1)
    if fmt == "e4m3":
        byte = np.frexp(amax)[1] - 1 + 127 - 7
    else:
        mant, ex = np.frexp(amax / 6.0)
        byte = np.where(mant > 0.5, ex, ex - 1) + 127
    byte = np.clip(np.where(amax > 0, byte, 1), 1, 254)
    scaled = (w * np.exp2(127.0 - byte)[:, None, :]).reshape(k, n).astype(np.float32)
    by_word = np.ascontiguousarray(scaled.reshape(k // 512, 128, 4, n).transpose(0, 1, 3, 2))
    if fmt == "e4m3":
        words = by_word.astype(ml_dtypes.float8_e4m3fn).view(np.uint8)
    else:
        c = by_word.astype(ml_dtypes.float4_e2m1fn).view(np.uint8) & 0xF
        words = (c[..., 0::2] | (c[..., 1::2] << 4)).reshape(k // 512, 128, 2 * n)
    return np.ascontiguousarray(words), np.ascontiguousarray(byte.astype(np.uint8).reshape(k // 512, 16, n))


def unpack_weight(words, scales, fmt):
    g, _, n = scales.shape
    words = np.ascontiguousarray(words).reshape(g, 128, n, -1)
    if fmt == "e4m3":
        vals = words.view(ml_dtypes.float8_e4m3fn).astype(np.float64)
    else:
        nib = np.empty((g, 128, n, 4), np.uint8)
        nib[..., 0::2] = words & 0xF
        nib[..., 1::2] = words >> 4
        vals = E2M1[nib]
    vals = vals * np.repeat(np.exp2(scales.astype(np.float64) - 127.0), 8, axis=1)[..., None]
    return vals.transpose(0, 1, 3, 2).reshape(g * 512, n)


K, J, R, T, F, C, N, S = 512, 384, 512, 2048, 1024, 512, 256, 1024


def setup_inputs():
    n = np.random.standard_normal
    idx = np.random.permutation(T)[:J]
    idx2 = np.random.permutation(F)[:R]
    idx3 = np.stack([np.random.permutation(C)[:J] for _ in range(8)])
    idx4 = np.stack([np.random.permutation(C)[:J] for _ in range(8)])
    idx5 = np.stack([np.random.permutation(C)[:J] for _ in range(8)])
    idx6 = np.random.permutation(S)[:N]
    fk = mx_kscale(K)
    fr = mx_kscale(R)
    tr = np.ones(F)
    tr[idx2] = fr
    xtp = pack_weight(n((K, T)) * fk[:, None], "e4m3")
    wtp = pack_weight(n((K, F)) * 1 / np.sqrt(K) / fk[:, None] * tr, "e2m1")
    vsp = pack_weight(n((R, S)) * 1 / np.sqrt(R) / fr[:, None], "e4m3")
    return {
        "xt_words": xtp[0],
        "xt_scales": xtp[1],
        "wt_words": wtp[0],
        "wt_scales": wtp[1],
        "vs_words": vsp[0],
        "vs_scales": vsp[1],
        "offs": striped(idx),
        "offs2": striped(idx2),
        "offs3": striped8(idx3),
        "offs4": striped8(idx4),
        "offs5": striped8(idx5),
        "offs6": striped(idx6),
    }


def reference(xt_words, xt_scales, wt_words, wt_scales, vs_words, vs_scales, offs, offs2, offs3, offs4, offs5, offs6):
    idx = unstriped(offs)
    idx2 = unstriped(offs2)
    idx3 = unstriped8(offs3)
    idx4 = unstriped8(offs4)
    idx5 = unstriped8(offs5)
    idx6 = unstriped(offs6)
    xtu = unpack_weight(xt_words, xt_scales, "e4m3")
    wtu = unpack_weight(wt_words, wt_scales, "e2m1")
    vsu = unpack_weight(vs_words, vs_scales, "e4m3")
    wtidx2g = wtu[:, idx2]
    xtidxg = xtu[:, idx]
    a = wtidx2g.T @ xtidxg
    pw = np.zeros((R, C))
    pw[np.arange(R)[:, None], idx3[np.arange(R) % 512 // 64]] = a
    pv = np.zeros((R, C))
    pv[np.arange(R)[:, None], idx4[np.arange(R) % 512 // 64]] = a
    pu = np.zeros((R, C))
    pu[np.arange(R)[:, None], idx5[np.arange(R) % 512 // 64]] = a
    hid = np.maximum(np.minimum(pw, pv), np.minimum(np.maximum(pw, pv), pu))
    vsidx6g = vsu[:, idx6]
    hidq = mxq(hid, 0, "e4m3")
    y = vsidx6g.T @ hidq
    return y

@@ -1,0 +1,157 @@
+from contextlib import ExitStack
+
+import concourse.mybir as mybir
+
+F32 = mybir.dt.float32
+BF16 = mybir.dt.bfloat16
+I32 = mybir.dt.int32
+U32 = mybir.dt.uint32
+U16 = mybir.dt.uint16
+U8 = mybir.dt.uint8
+FP8X4 = mybir.dt.float8_e4m3fn_x4
+FP4X4 = mybir.dt.float4_e2m1fn_x4
+COPY = mybir.ActivationFunctionType.Copy
+MIN = mybir.AluOpType.min
+MAX = mybir.AluOpType.max
+
+K, J, R, T, F, C, N, S = 512, 384, 512, 2048, 1024, 512, 256, 1024
+P = 128
+PACK = 4
+HALF = C // 2
+FLOPS = 2 * K * R * J + 2 * R * N * C
+
+
+def load_scale_rows(queue, plane, scales):
+    rows = scales[0].bitcast(I32)
+    for q in range(4):
+        queue.dma_start(out=plane[32 * q : 32 * q + 4, :].bitcast(I32), in_=rows[4 * q : 4 * q + 4, :])
+
+
+def tile_picked_tokens_store_one_medianboards_store_plain_kernel(
+    tc, xt_words, xt_scales, wt_words, wt_scales, vs_words, vs_scales, offs, offs2, offs3, offs4, offs5, offs6, out
+):
+    nc = tc.nc
+    with ExitStack() as ctx:
+        lists = ctx.enter_context(tc.tile_pool(name="lists", bufs=1))
+        keep = ctx.enter_context(tc.tile_pool(name="keep", bufs=1))
+        work = ctx.enter_context(tc.tile_pool(name="work", bufs=2))
+        psum = ctx.enter_context(tc.psum_pool(name="psum", bufs=1))
+
+        tok_list = lists.tile([P, J // 16], U16, name="tok_list")
+        feat_list = lists.tile([P, R // 16], U16, name="feat_list")
+        board_lists = [lists.tile([P, J // 16], U16, name="board_list%d" % b) for b in range(3)]
+        outf_list = lists.tile([P, N // 16], U16, name="outf_list")
+
+        wt_w = keep.tile([P, F], U16, name="wt_w", align_bytes=64)
+        wt_s = keep.tile([P, F], U8, name="wt_s", align_bytes=64)
+        xt_w = keep.tile([P, T], U32, name="xt_w", align_bytes=64)
+        xt_s = keep.tile([P, T], U8, name="xt_s", align_bytes=64)
+        vs_w = keep.tile([P, S], U32, name="vs_w", align_bytes=64)
+        vs_s = keep.tile([P, S], U8, name="vs_s", align_bytes=64)
+        boards = [keep.tile([P, C], F32, name="board%d" % b, align_bytes=64) for b in range(3)]
+
+        for plane in (wt_s, xt_s):
+            nc.vector.memset(plane[:].bitcast(I32), 0)
+        for board in boards:
+            nc.vector.memset(board[:], 0.0)
+        nc.vector.memset(vs_s[:].bitcast(I32), 0)
+
+        nc.sync.dma_start(feat_list[:], offs2)
+        nc.sync.dma_start(out=wt_w[:].bitcast(I32), in_=wt_words[0].bitcast(I32))
+        load_scale_rows(nc.scalar, wt_s, wt_scales)
+        nc.sync.dma_start(tok_list[:], offs)
+        nc.sync.dma_start(out=xt_w[:].bitcast(I32), in_=xt_words[0].rearrange("p n t -> p (n t)").bitcast(I32))
+        load_scale_rows(nc.scalar, xt_s, xt_scales)
+        for board_list, src in zip(board_lists, (offs3, offs4, offs5)):
+            nc.sync.dma_start(board_list[:], src)
+        nc.sync.dma_start(outf_list[:], offs6)
+        nc.sync.dma_start(out=vs_w[:].bitcast(I32), in_=vs_words[0].rearrange("p n t -> p (n t)").bitcast(I32))
+        load_scale_rows(nc.sync, vs_s, vs_scales)
+
+        wt_wg = keep.tile([P, R], U16, name="wt_wg", align_bytes=64)
+        wt_sg = keep.tile([P, R], U8, name="wt_sg", align_bytes=64)
+        xt_wg = keep.tile([P, J], U32, name="xt_wg", align_bytes=64)
+        xt_sg = keep.tile([P, J], U8, name="xt_sg", align_bytes=64)
+        nc.vector.tensor_copy(wt_wg[:], wt_w[:].indirect(feat_list[:]))
+        nc.vector.tensor_copy(wt_sg[:], wt_s[:].indirect(feat_list[:]))
+        nc.vector.tensor_copy(xt_sg[:], xt_s[:].indirect(tok_list[:]))
+
+        dealt_w = [keep.tile([P, 2 * P], U8, name="dealt_w%d" % t, align_bytes=64) for t in range(PACK)]
+        dealt_s = [keep.tile([P, P], U8, name="dealt_s%d" % t, align_bytes=64) for t in range(PACK)]
+        w_by_slot = wt_wg[:].bitcast(U8).rearrange("p (m t b) -> p t m b", t=PACK, b=2)
+        s_by_slot = wt_sg[:].rearrange("p (m t) -> p t m", t=PACK)
+
+        def deal(t):
+            nc.vector.tensor_copy(dealt_w[t][:].rearrange("p (m b) -> p m b", b=2), w_by_slot[:, t, :, :])
+            nc.vector.tensor_copy(dealt_s[t][:], s_by_slot[:, t, :])
+
+        deal(0)
+        nc.vector.tensor_copy(xt_wg[:], xt_w[:].indirect(tok_list[:]))
+
+        def first_product(t):
+            acc = psum.tile([P, J], F32, name="acc%d" % t)
+            for lo, hi in ((0, 256), (256, J)):
+                nc.tensor.matmul_mx(
+                    out=acc[:, lo:hi],
+                    lhsT=dealt_w[t][:].bitcast(FP4X4),
+                    lhsT_scale=dealt_s[t][:],
+                    rhs=xt_wg[:, lo:hi].bitcast(FP8X4),
+                    rhs_scale=xt_sg[:, lo:hi],
+                    start=True,
+                    stop=True,
+                )
+            a = keep.tile([P, J], F32, name="a%d" % t, align_bytes=64)
+            if t == 0:
+                nc.scalar.copy(a[:], acc[:])
+            else:
+                nc.vector.tensor_copy(a[:], acc[:])
+            return a
+
+        a_tiles = [first_product(0)]
+        for t in range(1, PACK):
+            deal(t)
+            a_tiles.append(first_product(t))
+
+        vs_wg = keep.tile([P, N], U32, name="vs_wg", align_bytes=64)
+        vs_sg = keep.tile([P, N], U8, name="vs_sg", align_bytes=64)
+        nc.vector.tensor_copy(vs_wg[:], vs_w[:].indirect(outf_list[:]))
+        nc.vector.tensor_copy(vs_sg[:], vs_s[:].indirect(outf_list[:]))
+
+        hid = [keep.tile([P, HALF, PACK], BF16, name="hid%d" % h, align_bytes=64) for h in range(2)]
+        for t in range(PACK):
+            for board, board_list in zip(boards, board_lists):
+                nc.scalar.activation(board[:].indirect(board_list[:]), a_tiles[t][:], COPY)
+            low = work.tile([P, C], F32, name="low")
+            high = work.tile([P, C], F32, name="high")
+            nc.vector.tensor_tensor(low[:], boards[0][:], boards[1][:], MIN)
+            nc.vector.tensor_tensor(high[:], boards[0][:], boards[1][:], MAX)
+            for h in range(2):
+                cols = slice(h * HALF, (h + 1) * HALF)
+                capped = work.tile([P, HALF], F32, name="capped")
+                nc.vector.tensor_tensor(capped[:], high[:, cols], boards[2][:, cols], MIN)
+                nc.vector.tensor_tensor(hid[h][:, :, t], low[:, cols], capped[:], MAX)
+
+        out_rows = out.rearrange("(a p) c -> p a c", p=P)
+        for h in range(2):
+            cols = slice(h * HALF, (h + 1) * HALF)
+            codes = keep.tile([P, HALF], U32, name="codes%d" % h, align_bytes=64)
+            plane = keep.tile([P, HALF], U8, name="plane%d" % h, align_bytes=64)
+            nc.vector.quantize_mx(out=codes[:].bitcast(FP8X4), scales=plane[:], in_=hid[h][:].rearrange("p c t -> p (c t)"))
+            for a in range(N // P):
+                y = psum.tile([P, HALF], F32, name="y%d%d" % (h, a))
+                nc.tensor.matmul_mx(
+                    out=y[:],
+                    lhsT=vs_wg[:, a * P : (a + 1) * P].bitcast(FP8X4),
+                    lhsT_scale=vs_sg[:, a * P : (a + 1) * P],
+                    rhs=codes[:].bitcast(FP8X4),
+                    rhs_scale=plane[:],
+                    start=True,
+                    stop=True,
+                )
+                res = keep.tile([P, HALF], F32, name="res%d%d" % (h, a), align_bytes=64)
+                if h == 1 and a == 1:
+                    nc.vector.tensor_copy(res[:], y[:])
+                    nc.sync.dma_start(out=out_rows[:, a, cols], in_=res[:])
+                else:
+                    nc.scalar.copy(res[:], y[:])
+                    (nc.scalar if h == 1 else nc.sync).dma_start(out=out_rows[:, a, cols], in_=res[:])

@@ -18,6 +18,8 @@ K, J, R, T, F, C, N, S = 512, 384, 512, 2048, 1024, 512, 256, 1024
 P = 128
 PACK = 4
 HALF = C // 2
+FIRST = 128
+PIECES = (slice(0, 128), slice(128, 384), slice(384, 512))
 FLOPS = 2 * K * R * J + 2 * R * N * C
 
 
@@ -43,104 +45,120 @@ def tile_picked_tokens_store_one_medianboards_store_plain_kernel(
         outf_list = lists.tile([P, N // 16], U16, name="outf_list")
 
         wt_w = keep.tile([P, F], U16, name="wt_w", align_bytes=64)
-        wt_s = keep.tile([P, F], U8, name="wt_s", align_bytes=64)
-        xt_w = keep.tile([P, T], U32, name="xt_w", align_bytes=64)
-        xt_s = keep.tile([P, T], U8, name="xt_s", align_bytes=64)
-        vs_w = keep.tile([P, S], U32, name="vs_w", align_bytes=64)
+        wt_s = keep.tile([P, F], U8, name="wt_s", tag="wt_s", align_bytes=64)
+        xt_w = keep.tile([P, T], U32, name="xt_w", tag="e4m3_words", align_bytes=64)
+        xt_s = keep.tile([P, T], U8, name="xt_s", tag="xt_s", align_bytes=64)
         vs_s = keep.tile([P, S], U8, name="vs_s", align_bytes=64)
         boards = [keep.tile([P, C], F32, name="board%d" % b, align_bytes=64) for b in range(3)]
 
         for plane in (wt_s, xt_s):
             nc.vector.memset(plane[:].bitcast(I32), 0)
         for board in boards:
-            nc.vector.memset(board[:], 0.0)
+            nc.vector.memset(board[:].bitcast(I32), 0)
         nc.vector.memset(vs_s[:].bitcast(I32), 0)
 
-        nc.sync.dma_start(feat_list[:], offs2)
         nc.sync.dma_start(out=wt_w[:].bitcast(I32), in_=wt_words[0].bitcast(I32))
-        load_scale_rows(nc.scalar, wt_s, wt_scales)
+        nc.sync.dma_start(feat_list[:], offs2)
+        load_scale_rows(nc.sync, wt_s, wt_scales)
         nc.sync.dma_start(tok_list[:], offs)
         nc.sync.dma_start(out=xt_w[:].bitcast(I32), in_=xt_words[0].rearrange("p n t -> p (n t)").bitcast(I32))
-        load_scale_rows(nc.scalar, xt_s, xt_scales)
+        load_scale_rows(nc.sync, xt_s, xt_scales)
         for board_list, src in zip(board_lists, (offs3, offs4, offs5)):
             nc.sync.dma_start(board_list[:], src)
         nc.sync.dma_start(outf_list[:], offs6)
-        nc.sync.dma_start(out=vs_w[:].bitcast(I32), in_=vs_words[0].rearrange("p n t -> p (n t)").bitcast(I32))
         load_scale_rows(nc.sync, vs_s, vs_scales)
 
         wt_wg = keep.tile([P, R], U16, name="wt_wg", align_bytes=64)
         wt_sg = keep.tile([P, R], U8, name="wt_sg", align_bytes=64)
-        xt_wg = keep.tile([P, J], U32, name="xt_wg", align_bytes=64)
         xt_sg = keep.tile([P, J], U8, name="xt_sg", align_bytes=64)
         nc.vector.tensor_copy(wt_wg[:], wt_w[:].indirect(feat_list[:]))
         nc.vector.tensor_copy(wt_sg[:], wt_s[:].indirect(feat_list[:]))
-        nc.vector.tensor_copy(xt_sg[:], xt_s[:].indirect(tok_list[:]))
 
-        dealt_w = [keep.tile([P, 2 * P], U8, name="dealt_w%d" % t, align_bytes=64) for t in range(PACK)]
-        dealt_s = [keep.tile([P, P], U8, name="dealt_s%d" % t, align_bytes=64) for t in range(PACK)]
+        dealt_w, dealt_s = {}, {}
         w_by_slot = wt_wg[:].bitcast(U8).rearrange("p (m t b) -> p t m b", t=PACK, b=2)
         s_by_slot = wt_sg[:].rearrange("p (m t) -> p t m", t=PACK)
 
         def deal(t):
+            dealt_w[t] = keep.tile([P, 2 * P], U8, name="dealt_w", align_bytes=64)
+            dealt_s[t] = keep.tile([P, P], U8, name="dealt_s", align_bytes=64)
             nc.vector.tensor_copy(dealt_w[t][:].rearrange("p (m b) -> p m b", b=2), w_by_slot[:, t, :, :])
             nc.vector.tensor_copy(dealt_s[t][:], s_by_slot[:, t, :])
 
         deal(0)
-        nc.vector.tensor_copy(xt_wg[:], xt_w[:].indirect(tok_list[:]))
+        slot_parts = (slice(0, FIRST), slice(FIRST, J))
 
-        def first_product(t):
-            acc = psum.tile([P, J], F32, name="acc%d" % t)
-            for lo, hi in ((0, 256), (256, J)):
-                nc.tensor.matmul_mx(
-                    out=acc[:, lo:hi],
-                    lhsT=dealt_w[t][:].bitcast(FP4X4),
-                    lhsT_scale=dealt_s[t][:],
-                    rhs=xt_wg[:, lo:hi].bitcast(FP8X4),
-                    rhs_scale=xt_sg[:, lo:hi],
-                    start=True,
-                    stop=True,
-                )
-            a = keep.tile([P, J], F32, name="a%d" % t, align_bytes=64)
-            if t == 0:
-                nc.scalar.copy(a[:], acc[:])
+        def list_columns(part):
+            return slice(part.start // 16, part.stop // 16)
+
+        def product(t, part, acc):
+            nc.tensor.matmul_mx(
+                out=acc,
+                lhsT=dealt_w[t][:].bitcast(FP4X4),
+                lhsT_scale=dealt_s[t][:],
+                rhs=xt_wg[part.start][:].bitcast(FP8X4),
+                rhs_scale=xt_sg[:, part],
+                start=True,
+                stop=True,
+            )
+
+        a_tiles = [keep.tile([P, J], F32, name="a%d" % t, align_bytes=64) for t in range(PACK)]
+        xt_wg = {}
+        for i, part in enumerate(slot_parts):
+            xt_wg[part.start] = keep.tile([P, part.stop - part.start], U32, name="xt_wg%d" % i, tag=("xt_wg0", "xt_s")[i], align_bytes=64)
+            nc.vector.tensor_copy(xt_wg[part.start][:], xt_w[:].indirect(tok_list[:, list_columns(part)]))
+            if i == 0:
+                nc.vector.tensor_copy(xt_sg[:], xt_s[:].indirect(tok_list[:]))
+            acc = psum.tile([P, part.stop - part.start], F32, name="acc", bufs=3)
+            product(0, part, acc[:])
+            if i == 0:
+                nc.scalar.copy(a_tiles[0][:, part], acc[:])
             else:
-                nc.vector.tensor_copy(a[:], acc[:])
-            return a
-
-        a_tiles = [first_product(0)]
+                nc.vector.tensor_copy(a_tiles[0][:, part], acc[:])
         for t in range(1, PACK):
             deal(t)
-            a_tiles.append(first_product(t))
+            acc = psum.tile([P, J], F32, name="acc", bufs=3)
+            for part in slot_parts:
+                product(t, part, acc[:, part])
+            nc.vector.tensor_copy(a_tiles[t][:], acc[:])
 
+        vs_w = keep.tile([P, S], U32, name="vs_w", tag="e4m3_words", align_bytes=64)
+        nc.sync.dma_start(out=vs_w[:].bitcast(I32), in_=vs_words[0].rearrange("p n t -> p (n t)").bitcast(I32))
         vs_wg = keep.tile([P, N], U32, name="vs_wg", align_bytes=64)
         vs_sg = keep.tile([P, N], U8, name="vs_sg", align_bytes=64)
         nc.vector.tensor_copy(vs_wg[:], vs_w[:].indirect(outf_list[:]))
         nc.vector.tensor_copy(vs_sg[:], vs_s[:].indirect(outf_list[:]))
 
-        hid = [keep.tile([P, HALF, PACK], BF16, name="hid%d" % h, align_bytes=64) for h in range(2)]
+        pairs = [keep.tile([P, 2, cols.stop - cols.start, 2], BF16, name="pairs%d" % h, align_bytes=64) for h, cols in enumerate(PIECES)]
         for t in range(PACK):
-            for board, board_list in zip(boards, board_lists):
-                nc.scalar.activation(board[:].indirect(board_list[:]), a_tiles[t][:], COPY)
+            for b, (board, board_list) in enumerate(zip(boards, board_lists)):
+                for part in slot_parts if t == 0 and b == 0 else (slice(0, J),):
+                    nc.scalar.activation(board[:].indirect(board_list[:, list_columns(part)]), a_tiles[t][:, part], COPY)
             low = work.tile([P, C], F32, name="low")
             high = work.tile([P, C], F32, name="high")
             nc.vector.tensor_tensor(low[:], boards[0][:], boards[1][:], MIN)
             nc.vector.tensor_tensor(high[:], boards[0][:], boards[1][:], MAX)
-            for h in range(2):
-                cols = slice(h * HALF, (h + 1) * HALF)
-                capped = work.tile([P, HALF], F32, name="capped")
+            for h, cols in enumerate(PIECES):
+                capped = work.tile([P, cols.stop - cols.start], F32, name="capped%d" % h)
                 nc.vector.tensor_tensor(capped[:], high[:, cols], boards[2][:, cols], MIN)
-                nc.vector.tensor_tensor(hid[h][:, :, t], low[:, cols], capped[:], MAX)
+                nc.vector.tensor_tensor(pairs[h][:, t // 2, :, t % 2], low[:, cols], capped[:], MAX)
 
         out_rows = out.rearrange("(a p) c -> p a c", p=P)
-        for h in range(2):
-            cols = slice(h * HALF, (h + 1) * HALF)
-            codes = keep.tile([P, HALF], U32, name="codes%d" % h, align_bytes=64)
-            plane = keep.tile([P, HALF], U8, name="plane%d" % h, align_bytes=64)
-            nc.vector.quantize_mx(out=codes[:].bitcast(FP8X4), scales=plane[:], in_=hid[h][:].rearrange("p c t -> p (c t)"))
-            for a in range(N // P):
-                y = psum.tile([P, HALF], F32, name="y%d%d" % (h, a))
+        for h, cols in enumerate(PIECES):
+            width = cols.stop - cols.start
+            hid = keep.tile([P, width * PACK], BF16, name="hid%d" % h, align_bytes=64)
+            woven = hid[:].bitcast(F32).rearrange("p (c u) -> p c u", u=2)
+            apart = pairs[h][:].rearrange("p u c e -> p (u c e)").bitcast(F32).rearrange("p (u c) -> p c u", u=2)
+            if h < 2:
+                nc.scalar.copy(woven, apart)
+            else:
+                nc.vector.tensor_copy(woven, apart)
+            codes = keep.tile([P, width], U32, name="codes%d" % h, align_bytes=64)
+            plane = keep.tile([P, width], U8, name="plane%d" % h, align_bytes=64)
+            nc.vector.quantize_mx(out=codes[:].bitcast(FP8X4), scales=plane[:], in_=hid[:])
+
+            def second(a, y):
                 nc.tensor.matmul_mx(
-                    out=y[:],
+                    out=y,
                     lhsT=vs_wg[:, a * P : (a + 1) * P].bitcast(FP8X4),
                     lhsT_scale=vs_sg[:, a * P : (a + 1) * P],
                     rhs=codes[:].bitcast(FP8X4),
@@ -148,10 +166,22 @@ def tile_picked_tokens_store_one_medianboards_store_plain_kernel(
                     start=True,
                     stop=True,
                 )
-                res = keep.tile([P, HALF], F32, name="res%d%d" % (h, a), align_bytes=64)
-                if h == 1 and a == 1:
-                    nc.vector.tensor_copy(res[:], y[:])
-                    nc.sync.dma_start(out=out_rows[:, a, cols], in_=res[:])
-                else:
-                    nc.scalar.copy(res[:], y[:])
-                    (nc.scalar if h == 1 else nc.sync).dma_start(out=out_rows[:, a, cols], in_=res[:])
+
+            if h == 0:
+                y = psum.tile([P, 2, width], F32, name="y0")
+                res = keep.tile([P, 2, width], F32, name="res0")
+                for a in range(2):
+                    second(a, y[:, a, :])
+                nc.scalar.copy(res[:], y[:])
+                nc.sync.dma_start(out=out_rows[:, :, cols], in_=res[:])
+            else:
+                for a in range(2):
+                    y = psum.tile([P, width], F32, name="y%d%d" % (h, a))
+                    res = keep.tile([P, width], F32, name="res%d%d" % (h, a))
+                    second(a, y[:])
+                    if a == 0:
+                        nc.scalar.copy(res[:], y[:])
+                    else:
+                        nc.vector.tensor_copy(res[:], y[:])
+                    store_queue = nc.scalar if h == 2 and a == 0 else nc.sync
+                    store_queue.dma_start(out=out_rows[:, a, cols], in_=res[:])

@@ -17,16 +17,29 @@ MAX = mybir.AluOpType.max
 K, J, R, T, F, C, N, S = 512, 384, 512, 2048, 1024, 512, 256, 1024
 P = 128
 PACK = 4
-HALF = C // 2
-FIRST = 128
-PIECES = (slice(0, 128), slice(128, 384), slice(384, 512))
+GROUP = 16
+BOARDS = 3
+SLOT_PARTS = (slice(0, 128), slice(128, J))
+PIECES = (slice(0, 128), slice(128, 384), slice(384, C))
 FLOPS = 2 * K * R * J + 2 * R * N * C
 
 
-def load_scale_rows(queue, plane, scales):
+def width_of(columns):
+    return columns.stop - columns.start
+
+
+def list_columns(slots):
+    return slice(slots.start // GROUP, slots.stop // GROUP)
+
+
+def load_scale_rows(nc, plane, scales):
     rows = scales[0].bitcast(I32)
     for q in range(4):
-        queue.dma_start(out=plane[32 * q : 32 * q + 4, :].bitcast(I32), in_=rows[4 * q : 4 * q + 4, :])
+        nc.sync.dma_start(out=plane[32 * q : 32 * q + 4, :].bitcast(I32), in_=rows[4 * q : 4 * q + 4, :])
+
+
+def load_e4m3_words(nc, tile, words):
+    nc.sync.dma_start(out=tile[:].bitcast(I32), in_=words[0].rearrange("p n t -> p (n t)").bitcast(I32))
 
 
 def tile_picked_tokens_store_one_medianboards_store_plain_kernel(
@@ -36,20 +49,20 @@ def tile_picked_tokens_store_one_medianboards_store_plain_kernel(
     with ExitStack() as ctx:
         lists = ctx.enter_context(tc.tile_pool(name="lists", bufs=1))
         keep = ctx.enter_context(tc.tile_pool(name="keep", bufs=1))
-        work = ctx.enter_context(tc.tile_pool(name="work", bufs=2))
+        ring = ctx.enter_context(tc.tile_pool(name="ring", bufs=2))
         psum = ctx.enter_context(tc.psum_pool(name="psum", bufs=1))
 
-        tok_list = lists.tile([P, J // 16], U16, name="tok_list")
-        feat_list = lists.tile([P, R // 16], U16, name="feat_list")
-        board_lists = [lists.tile([P, J // 16], U16, name="board_list%d" % b) for b in range(3)]
-        outf_list = lists.tile([P, N // 16], U16, name="outf_list")
+        token_list = lists.tile([P, J // GROUP], U16, name="token_list")
+        feature_list = lists.tile([P, R // GROUP], U16, name="feature_list")
+        board_lists = [lists.tile([P, J // GROUP], U16, name="board_list%d" % b) for b in range(BOARDS)]
+        output_list = lists.tile([P, N // GROUP], U16, name="output_list")
 
         wt_w = keep.tile([P, F], U16, name="wt_w", align_bytes=64)
-        wt_s = keep.tile([P, F], U8, name="wt_s", tag="wt_s", align_bytes=64)
-        xt_w = keep.tile([P, T], U32, name="xt_w", tag="e4m3_words", align_bytes=64)
+        wt_s = keep.tile([P, F], U8, name="wt_s", align_bytes=64)
+        xt_w = keep.tile([P, T], U32, name="xt_w", tag="e4m3_table", align_bytes=64)
         xt_s = keep.tile([P, T], U8, name="xt_s", tag="xt_s", align_bytes=64)
         vs_s = keep.tile([P, S], U8, name="vs_s", align_bytes=64)
-        boards = [keep.tile([P, C], F32, name="board%d" % b, align_bytes=64) for b in range(3)]
+        boards = [keep.tile([P, C], F32, name="board%d" % b, align_bytes=64) for b in range(BOARDS)]
 
         for plane in (wt_s, xt_s):
             nc.vector.memset(plane[:].bitcast(I32), 0)
@@ -58,130 +71,145 @@ def tile_picked_tokens_store_one_medianboards_store_plain_kernel(
         nc.vector.memset(vs_s[:].bitcast(I32), 0)
 
         nc.sync.dma_start(out=wt_w[:].bitcast(I32), in_=wt_words[0].bitcast(I32))
-        nc.sync.dma_start(feat_list[:], offs2)
-        load_scale_rows(nc.sync, wt_s, wt_scales)
-        nc.sync.dma_start(tok_list[:], offs)
-        nc.sync.dma_start(out=xt_w[:].bitcast(I32), in_=xt_words[0].rearrange("p n t -> p (n t)").bitcast(I32))
-        load_scale_rows(nc.sync, xt_s, xt_scales)
-        for board_list, src in zip(board_lists, (offs3, offs4, offs5)):
-            nc.sync.dma_start(board_list[:], src)
-        nc.sync.dma_start(outf_list[:], offs6)
-        load_scale_rows(nc.sync, vs_s, vs_scales)
+        nc.sync.dma_start(feature_list[:], offs2)
+        load_scale_rows(nc, wt_s, wt_scales)
+        nc.sync.dma_start(token_list[:], offs)
+        load_e4m3_words(nc, xt_w, xt_words)
+        load_scale_rows(nc, xt_s, xt_scales)
+        for board_list, board_offs in zip(board_lists, (offs3, offs4, offs5)):
+            nc.sync.dma_start(board_list[:], board_offs)
+        nc.sync.dma_start(output_list[:], offs6)
+        load_scale_rows(nc, vs_s, vs_scales)
 
         wt_wg = keep.tile([P, R], U16, name="wt_wg", align_bytes=64)
         wt_sg = keep.tile([P, R], U8, name="wt_sg", align_bytes=64)
         xt_sg = keep.tile([P, J], U8, name="xt_sg", align_bytes=64)
-        nc.vector.tensor_copy(wt_wg[:], wt_w[:].indirect(feat_list[:]))
-        nc.vector.tensor_copy(wt_sg[:], wt_s[:].indirect(feat_list[:]))
+        nc.vector.tensor_copy(wt_wg[:], wt_w[:].indirect(feature_list[:]))
+        nc.vector.tensor_copy(wt_sg[:], wt_s[:].indirect(feature_list[:]))
 
         dealt_w, dealt_s = {}, {}
-        w_by_slot = wt_wg[:].bitcast(U8).rearrange("p (m t b) -> p t m b", t=PACK, b=2)
-        s_by_slot = wt_sg[:].rearrange("p (m t) -> p t m", t=PACK)
+        w_by_row_tile = wt_wg[:].bitcast(U8).rearrange("p (m t b) -> p t m b", t=PACK, b=2)
+        s_by_row_tile = wt_sg[:].rearrange("p (m t) -> p t m", t=PACK)
 
-        def deal(t):
-            dealt_w[t] = keep.tile([P, 2 * P], U8, name="dealt_w", align_bytes=64)
-            dealt_s[t] = keep.tile([P, P], U8, name="dealt_s", align_bytes=64)
-            nc.vector.tensor_copy(dealt_w[t][:].rearrange("p (m b) -> p m b", b=2), w_by_slot[:, t, :, :])
-            nc.vector.tensor_copy(dealt_s[t][:], s_by_slot[:, t, :])
+        def deal(first, last):
+            words = keep.tile([P, last - first, P, 2], U8, name="dealt_w", align_bytes=64)
+            scales = keep.tile([P, last - first, P], U8, name="dealt_s", align_bytes=64)
+            nc.vector.tensor_copy(words[:], w_by_row_tile[:, first:last, :, :])
+            nc.vector.tensor_copy(scales[:], s_by_row_tile[:, first:last, :])
+            for t in range(first, last):
+                dealt_w[t] = words[:, t - first, :, :].rearrange("p m b -> p (m b)")
+                dealt_s[t] = scales[:, t - first, :]
 
-        deal(0)
-        slot_parts = (slice(0, FIRST), slice(FIRST, J))
+        xt_wg = []
 
-        def list_columns(part):
-            return slice(part.start // 16, part.stop // 16)
+        def gather_token_words(tag):
+            slots = SLOT_PARTS[len(xt_wg)]
+            words = keep.tile([P, width_of(slots)], U32, name="xt_wg%d" % len(xt_wg), tag=tag, align_bytes=64)
+            nc.vector.tensor_copy(words[:], xt_w[:].indirect(token_list[:, list_columns(slots)]))
+            xt_wg.append(words)
 
-        def product(t, part, acc):
+        def first_product(t, part, acc):
             nc.tensor.matmul_mx(
                 out=acc,
-                lhsT=dealt_w[t][:].bitcast(FP4X4),
-                lhsT_scale=dealt_s[t][:],
-                rhs=xt_wg[part.start][:].bitcast(FP8X4),
-                rhs_scale=xt_sg[:, part],
+                lhsT=dealt_w[t].bitcast(FP4X4),
+                lhsT_scale=dealt_s[t],
+                rhs=xt_wg[part][:].bitcast(FP8X4),
+                rhs_scale=xt_sg[:, SLOT_PARTS[part]],
                 start=True,
                 stop=True,
             )
 
+        def product_bank(width):
+            return psum.tile([P, width], F32, name="acc", bufs=3)
+
         a_tiles = [keep.tile([P, J], F32, name="a%d" % t, align_bytes=64) for t in range(PACK)]
-        xt_wg = {}
-        for i, part in enumerate(slot_parts):
-            xt_wg[part.start] = keep.tile([P, part.stop - part.start], U32, name="xt_wg%d" % i, tag=("xt_wg0", "xt_s")[i], align_bytes=64)
-            nc.vector.tensor_copy(xt_wg[part.start][:], xt_w[:].indirect(tok_list[:, list_columns(part)]))
-            if i == 0:
-                nc.vector.tensor_copy(xt_sg[:], xt_s[:].indirect(tok_list[:]))
-            acc = psum.tile([P, part.stop - part.start], F32, name="acc", bufs=3)
-            product(0, part, acc[:])
-            if i == 0:
-                nc.scalar.copy(a_tiles[0][:, part], acc[:])
-            else:
-                nc.vector.tensor_copy(a_tiles[0][:, part], acc[:])
+        deal(0, 1)
+        gather_token_words("xt_wg0")
+        nc.vector.tensor_copy(xt_sg[:], xt_s[:].indirect(token_list[:]))
+        acc = product_bank(width_of(SLOT_PARTS[0]))
+        first_product(0, 0, acc[:])
+        nc.scalar.copy(a_tiles[0][:, SLOT_PARTS[0]], acc[:])
+
+        gather_token_words("xt_s")
+        acc = product_bank(width_of(SLOT_PARTS[1]))
+        first_product(0, 1, acc[:])
+        nc.vector.tensor_copy(a_tiles[0][:, SLOT_PARTS[1]], acc[:])
+
+        deal(1, PACK)
         for t in range(1, PACK):
-            deal(t)
-            acc = psum.tile([P, J], F32, name="acc", bufs=3)
-            for part in slot_parts:
-                product(t, part, acc[:, part])
+            acc = product_bank(J)
+            for part, slots in enumerate(SLOT_PARTS):
+                first_product(t, part, acc[:, slots])
             nc.vector.tensor_copy(a_tiles[t][:], acc[:])
 
-        vs_w = keep.tile([P, S], U32, name="vs_w", tag="e4m3_words", align_bytes=64)
-        nc.sync.dma_start(out=vs_w[:].bitcast(I32), in_=vs_words[0].rearrange("p n t -> p (n t)").bitcast(I32))
-        vs_wg = keep.tile([P, N], U32, name="vs_wg", align_bytes=64)
-        vs_sg = keep.tile([P, N], U8, name="vs_sg", align_bytes=64)
-        nc.vector.tensor_copy(vs_wg[:], vs_w[:].indirect(outf_list[:]))
-        nc.vector.tensor_copy(vs_sg[:], vs_s[:].indirect(outf_list[:]))
+        vs_w = keep.tile([P, S], U32, name="vs_w", tag="e4m3_table", align_bytes=64)
+        load_e4m3_words(nc, vs_w, vs_words)
 
-        pairs = [keep.tile([P, 2, cols.stop - cols.start, 2], BF16, name="pairs%d" % h, align_bytes=64) for h, cols in enumerate(PIECES)]
+        pairs = [
+            keep.tile([P, 2, width_of(cols), 2], BF16, name="pairs%d" % h, align_bytes=64)
+            for h, cols in enumerate(PIECES)
+        ]
         for t in range(PACK):
-            for b, (board, board_list) in enumerate(zip(boards, board_lists)):
-                for part in slot_parts if t == 0 and b == 0 else (slice(0, J),):
-                    nc.scalar.activation(board[:].indirect(board_list[:, list_columns(part)]), a_tiles[t][:, part], COPY)
-            low = work.tile([P, C], F32, name="low")
-            high = work.tile([P, C], F32, name="high")
+            for slots in SLOT_PARTS if t == 0 else (slice(0, J),):
+                for board, board_list in zip(boards, board_lists):
+                    window = board[:].indirect(board_list[:, list_columns(slots)])
+                    nc.scalar.activation(window, a_tiles[t][:, slots], COPY)
+            low = keep.tile([P, C], F32, name="low", tag="dealt_w", align_bytes=64)
+            high = keep.tile([P, C], F32, name="high", tag="dealt_s", align_bytes=64)
             nc.vector.tensor_tensor(low[:], boards[0][:], boards[1][:], MIN)
             nc.vector.tensor_tensor(high[:], boards[0][:], boards[1][:], MAX)
             for h, cols in enumerate(PIECES):
-                capped = work.tile([P, cols.stop - cols.start], F32, name="capped%d" % h)
+                capped = ring.tile([P, width_of(cols)], F32, name="capped%d" % h)
                 nc.vector.tensor_tensor(capped[:], high[:, cols], boards[2][:, cols], MIN)
                 nc.vector.tensor_tensor(pairs[h][:, t // 2, :, t % 2], low[:, cols], capped[:], MAX)
+            if t == 0:
+                vs_wg = keep.tile([P, N], U32, name="vs_wg", tag="xt_wg0", align_bytes=64)
+                vs_sg = keep.tile([P, N], U8, name="vs_sg", tag="xt_sg", align_bytes=64)
+                nc.vector.tensor_copy(vs_wg[:], vs_w[:].indirect(output_list[:]))
+                nc.vector.tensor_copy(vs_sg[:], vs_s[:].indirect(output_list[:]))
 
-        out_rows = out.rearrange("(a p) c -> p a c", p=P)
+        def second_product(half, codes, code_scales, y):
+            features = slice(half * P, (half + 1) * P)
+            nc.tensor.matmul_mx(
+                out=y,
+                lhsT=vs_wg[:, features].bitcast(FP8X4),
+                lhsT_scale=vs_sg[:, features],
+                rhs=codes[:].bitcast(FP8X4),
+                rhs_scale=code_scales[:],
+                start=True,
+                stop=True,
+            )
+
+        out_rows = out.rearrange("(half p) c -> p half c", p=P)
+        last_piece = len(PIECES) - 1
         for h, cols in enumerate(PIECES):
-            width = cols.stop - cols.start
+            width = width_of(cols)
             hid = keep.tile([P, width * PACK], BF16, name="hid%d" % h, align_bytes=64)
             woven = hid[:].bitcast(F32).rearrange("p (c u) -> p c u", u=2)
             apart = pairs[h][:].rearrange("p u c e -> p (u c e)").bitcast(F32).rearrange("p (u c) -> p c u", u=2)
-            if h < 2:
+            if h < last_piece:
                 nc.scalar.copy(woven, apart)
             else:
                 nc.vector.tensor_copy(woven, apart)
             codes = keep.tile([P, width], U32, name="codes%d" % h, align_bytes=64)
-            plane = keep.tile([P, width], U8, name="plane%d" % h, align_bytes=64)
-            nc.vector.quantize_mx(out=codes[:].bitcast(FP8X4), scales=plane[:], in_=hid[:])
-
-            def second(a, y):
-                nc.tensor.matmul_mx(
-                    out=y,
-                    lhsT=vs_wg[:, a * P : (a + 1) * P].bitcast(FP8X4),
-                    lhsT_scale=vs_sg[:, a * P : (a + 1) * P],
-                    rhs=codes[:].bitcast(FP8X4),
-                    rhs_scale=plane[:],
-                    start=True,
-                    stop=True,
-                )
+            code_scales = keep.tile([P, width], U8, name="code_scales%d" % h, align_bytes=64)
+            nc.vector.quantize_mx(out=codes[:].bitcast(FP8X4), scales=code_scales[:], in_=hid[:])
 
             if h == 0:
                 y = psum.tile([P, 2, width], F32, name="y0")
-                res = keep.tile([P, 2, width], F32, name="res0")
-                for a in range(2):
-                    second(a, y[:, a, :])
-                nc.scalar.copy(res[:], y[:])
-                nc.sync.dma_start(out=out_rows[:, :, cols], in_=res[:])
+                result = keep.tile([P, 2, width], F32, name="result0")
+                for half in range(2):
+                    second_product(half, codes, code_scales, y[:, half, :])
+                nc.scalar.copy(result[:], y[:])
+                nc.sync.dma_start(out=out_rows[:, :, cols], in_=result[:])
             else:
-                for a in range(2):
-                    y = psum.tile([P, width], F32, name="y%d%d" % (h, a))
-                    res = keep.tile([P, width], F32, name="res%d%d" % (h, a))
-                    second(a, y[:])
-                    if a == 0:
-                        nc.scalar.copy(res[:], y[:])
+                for half in range(2):
+                    y = psum.tile([P, width], F32, name="y%d%d" % (h, half))
+                    result = keep.tile([P, width], F32, name="result%d%d" % (h, half))
+                    second_product(half, codes, code_scales, y[:])
+                    if half == 0:
+                        nc.scalar.copy(result[:], y[:])
                     else:
-                        nc.vector.tensor_copy(res[:], y[:])
-                    store_queue = nc.scalar if h == 2 and a == 0 else nc.sync
-                    store_queue.dma_start(out=out_rows[:, a, cols], in_=res[:])
+                        nc.vector.tensor_copy(result[:], y[:])
+                    store_queue = nc.scalar if h == last_piece and half == 0 else nc.sync
+                    store_queue.dma_start(out=out_rows[:, half, cols], in_=result[:])

from contextlib import ExitStack

import concourse.mybir as mybir

F32 = mybir.dt.float32
BF16 = mybir.dt.bfloat16
I32 = mybir.dt.int32
U32 = mybir.dt.uint32
U16 = mybir.dt.uint16
U8 = mybir.dt.uint8
FP8X4 = mybir.dt.float8_e4m3fn_x4
FP4X4 = mybir.dt.float4_e2m1fn_x4
COPY = mybir.ActivationFunctionType.Copy
MIN = mybir.AluOpType.min
MAX = mybir.AluOpType.max

K, J, R, T, F, C, N, S = 512, 384, 512, 2048, 1024, 512, 256, 1024
P = 128
PACK = 4
GROUP = 16
BOARDS = 3
SLOT_PARTS = (slice(0, 128), slice(128, J))
PIECES = (slice(0, 128), slice(128, 384), slice(384, C))
FLOPS = 2 * K * R * J + 2 * R * N * C


def width_of(columns):
    return columns.stop - columns.start


def list_columns(slots):
    return slice(slots.start // GROUP, slots.stop // GROUP)


def load_scale_rows(nc, plane, scales):
    rows = scales[0].bitcast(I32)
    for q in range(4):
        nc.sync.dma_start(out=plane[32 * q : 32 * q + 4, :].bitcast(I32), in_=rows[4 * q : 4 * q + 4, :])


def load_e4m3_words(nc, tile, words):
    nc.sync.dma_start(out=tile[:].bitcast(I32), in_=words[0].rearrange("p n t -> p (n t)").bitcast(I32))


def tile_picked_tokens_store_one_medianboards_store_plain_kernel(
    tc, xt_words, xt_scales, wt_words, wt_scales, vs_words, vs_scales, offs, offs2, offs3, offs4, offs5, offs6, out
):
    nc = tc.nc
    with ExitStack() as ctx:
        lists = ctx.enter_context(tc.tile_pool(name="lists", bufs=1))
        keep = ctx.enter_context(tc.tile_pool(name="keep", bufs=1))
        ring = ctx.enter_context(tc.tile_pool(name="ring", bufs=2))
        psum = ctx.enter_context(tc.psum_pool(name="psum", bufs=1))

        token_list = lists.tile([P, J // GROUP], U16, name="token_list")
        feature_list = lists.tile([P, R // GROUP], U16, name="feature_list")
        board_lists = [lists.tile([P, J // GROUP], U16, name="board_list%d" % b) for b in range(BOARDS)]
        output_list = lists.tile([P, N // GROUP], U16, name="output_list")

        wt_w = keep.tile([P, F], U16, name="wt_w", align_bytes=64)
        wt_s = keep.tile([P, F], U8, name="wt_s", align_bytes=64)
        xt_w = keep.tile([P, T], U32, name="xt_w", tag="e4m3_table", align_bytes=64)
        xt_s = keep.tile([P, T], U8, name="xt_s", tag="xt_s", align_bytes=64)
        vs_s = keep.tile([P, S], U8, name="vs_s", align_bytes=64)
        boards = [keep.tile([P, C], F32, name="board%d" % b, align_bytes=64) for b in range(BOARDS)]

        for plane in (wt_s, xt_s):
            nc.vector.memset(plane[:].bitcast(I32), 0)
        for board in boards:
            nc.vector.memset(board[:].bitcast(I32), 0)
        nc.vector.memset(vs_s[:].bitcast(I32), 0)

        nc.sync.dma_start(out=wt_w[:].bitcast(I32), in_=wt_words[0].bitcast(I32))
        nc.sync.dma_start(feature_list[:], offs2)
        load_scale_rows(nc, wt_s, wt_scales)
        nc.sync.dma_start(token_list[:], offs)
        load_e4m3_words(nc, xt_w, xt_words)
        load_scale_rows(nc, xt_s, xt_scales)
        for board_list, board_offs in zip(board_lists, (offs3, offs4, offs5)):
            nc.sync.dma_start(board_list[:], board_offs)
        nc.sync.dma_start(output_list[:], offs6)
        load_scale_rows(nc, vs_s, vs_scales)

        wt_wg = keep.tile([P, R], U16, name="wt_wg", align_bytes=64)
        wt_sg = keep.tile([P, R], U8, name="wt_sg", align_bytes=64)
        xt_sg = keep.tile([P, J], U8, name="xt_sg", align_bytes=64)
        nc.vector.tensor_copy(wt_wg[:], wt_w[:].indirect(feature_list[:]))
        nc.vector.tensor_copy(wt_sg[:], wt_s[:].indirect(feature_list[:]))

        dealt_w, dealt_s = {}, {}
        w_by_row_tile = wt_wg[:].bitcast(U8).rearrange("p (m t b) -> p t m b", t=PACK, b=2)
        s_by_row_tile = wt_sg[:].rearrange("p (m t) -> p t m", t=PACK)

        def deal(first, last):
            words = keep.tile([P, last - first, P, 2], U8, name="dealt_w", align_bytes=64)
            scales = keep.tile([P, last - first, P], U8, name="dealt_s", align_bytes=64)
            nc.vector.tensor_copy(words[:], w_by_row_tile[:, first:last, :, :])
            nc.vector.tensor_copy(scales[:], s_by_row_tile[:, first:last, :])
            for t in range(first, last):
                dealt_w[t] = words[:, t - first, :, :].rearrange("p m b -> p (m b)")
                dealt_s[t] = scales[:, t - first, :]

        xt_wg = []

        def gather_token_words(tag):
            slots = SLOT_PARTS[len(xt_wg)]
            words = keep.tile([P, width_of(slots)], U32, name="xt_wg%d" % len(xt_wg), tag=tag, align_bytes=64)
            nc.vector.tensor_copy(words[:], xt_w[:].indirect(token_list[:, list_columns(slots)]))
            xt_wg.append(words)

        def first_product(t, part, acc):
            nc.tensor.matmul_mx(
                out=acc,
                lhsT=dealt_w[t].bitcast(FP4X4),
                lhsT_scale=dealt_s[t],
                rhs=xt_wg[part][:].bitcast(FP8X4),
                rhs_scale=xt_sg[:, SLOT_PARTS[part]],
                start=True,
                stop=True,
            )

        def product_bank(width):
            return psum.tile([P, width], F32, name="acc", bufs=3)

        a_tiles = [keep.tile([P, J], F32, name="a%d" % t, align_bytes=64) for t in range(PACK)]
        deal(0, 1)
        gather_token_words("xt_wg0")
        nc.vector.tensor_copy(xt_sg[:], xt_s[:].indirect(token_list[:]))
        acc = product_bank(width_of(SLOT_PARTS[0]))
        first_product(0, 0, acc[:])
        nc.scalar.copy(a_tiles[0][:, SLOT_PARTS[0]], acc[:])

        gather_token_words("xt_s")
        acc = product_bank(width_of(SLOT_PARTS[1]))
        first_product(0, 1, acc[:])
        nc.vector.tensor_copy(a_tiles[0][:, SLOT_PARTS[1]], acc[:])

        deal(1, PACK)
        for t in range(1, PACK):
            acc = product_bank(J)
            for part, slots in enumerate(SLOT_PARTS):
                first_product(t, part, acc[:, slots])
            nc.vector.tensor_copy(a_tiles[t][:], acc[:])

        vs_w = keep.tile([P, S], U32, name="vs_w", tag="e4m3_table", align_bytes=64)
        load_e4m3_words(nc, vs_w, vs_words)

        pairs = [
            keep.tile([P, 2, width_of(cols), 2], BF16, name="pairs%d" % h, align_bytes=64)
            for h, cols in enumerate(PIECES)
        ]
        for t in range(PACK):
            for slots in SLOT_PARTS if t == 0 else (slice(0, J),):
                for board, board_list in zip(boards, board_lists):
                    window = board[:].indirect(board_list[:, list_columns(slots)])
                    nc.scalar.activation(window, a_tiles[t][:, slots], COPY)
            low = keep.tile([P, C], F32, name="low", tag="dealt_w", align_bytes=64)
            high = keep.tile([P, C], F32, name="high", tag="dealt_s", align_bytes=64)
            nc.vector.tensor_tensor(low[:], boards[0][:], boards[1][:], MIN)
            nc.vector.tensor_tensor(high[:], boards[0][:], boards[1][:], MAX)
            for h, cols in enumerate(PIECES):
                capped = ring.tile([P, width_of(cols)], F32, name="capped%d" % h)
                nc.vector.tensor_tensor(capped[:], high[:, cols], boards[2][:, cols], MIN)
                nc.vector.tensor_tensor(pairs[h][:, t // 2, :, t % 2], low[:, cols], capped[:], MAX)
            if t == 0:
                vs_wg = keep.tile([P, N], U32, name="vs_wg", tag="xt_wg0", align_bytes=64)
                vs_sg = keep.tile([P, N], U8, name="vs_sg", tag="xt_sg", align_bytes=64)
                nc.vector.tensor_copy(vs_wg[:], vs_w[:].indirect(output_list[:]))
                nc.vector.tensor_copy(vs_sg[:], vs_s[:].indirect(output_list[:]))

        def second_product(half, codes, code_scales, y):
            features = slice(half * P, (half + 1) * P)
            nc.tensor.matmul_mx(
                out=y,
                lhsT=vs_wg[:, features].bitcast(FP8X4),
                lhsT_scale=vs_sg[:, features],
                rhs=codes[:].bitcast(FP8X4),
                rhs_scale=code_scales[:],
                start=True,
                stop=True,
            )

        out_rows = out.rearrange("(half p) c -> p half c", p=P)
        last_piece = len(PIECES) - 1
        for h, cols in enumerate(PIECES):
            width = width_of(cols)
            hid = keep.tile([P, width * PACK], BF16, name="hid%d" % h, align_bytes=64)
            woven = hid[:].bitcast(F32).rearrange("p (c u) -> p c u", u=2)
            apart = pairs[h][:].rearrange("p u c e -> p (u c e)").bitcast(F32).rearrange("p (u c) -> p c u", u=2)
            if h < last_piece:
                nc.scalar.copy(woven, apart)
            else:
                nc.vector.tensor_copy(woven, apart)
            codes = keep.tile([P, width], U32, name="codes%d" % h, align_bytes=64)
            code_scales = keep.tile([P, width], U8, name="code_scales%d" % h, align_bytes=64)
            nc.vector.quantize_mx(out=codes[:].bitcast(FP8X4), scales=code_scales[:], in_=hid[:])

            if h == 0:
                y = psum.tile([P, 2, width], F32, name="y0")
                result = keep.tile([P, 2, width], F32, name="result0")
                for half in range(2):
                    second_product(half, codes, code_scales, y[:, half, :])
                nc.scalar.copy(result[:], y[:])
                nc.sync.dma_start(out=out_rows[:, :, cols], in_=result[:])
            else:
                for half in range(2):
                    y = psum.tile([P, width], F32, name="y%d%d" % (h, half))
                    result = keep.tile([P, width], F32, name="result%d%d" % (h, half))
                    second_product(half, codes, code_scales, y[:])
                    if half == 0:
                        nc.scalar.copy(result[:], y[:])
                    else:
                        nc.vector.tensor_copy(result[:], y[:])
                    store_queue = nc.scalar if h == last_piece and half == 0 else nc.sync
                    store_queue.dma_start(out=out_rows[:, half, cols], in_=result[:])
